import numpy as np, ml_dtypes
CORES = [66,74,82,90,194,202,210,218]
N = 8
BF = ml_dtypes.bfloat16
def gentries(a):
    return np.ascontiguousarray(a.reshape(8, 16, -1).transpose(0, 2, 1)).reshape(8, -1)
def gtable(e):
    e = np.asarray(e); return np.ascontiguousarray(e.reshape(8, -1, 16).transpose(0, 2, 1)).reshape(128, -1).astype(np.int32)
W, R, PG, V, H = 4096, 16, 192, 5, 5
K = PG * R
def parts(rng):
    x = rng.integers(0, 256, (N, 8, 16, W)); e = rng.integers(0, 256, (N, 8, 16, PG)); w = rng.integers(0, 16, (N, 8, 16))
    h = rng.choice(np.array([1000, 1300, 1600, 1900]), (N, 8, 1)) + rng.integers(-300, 301, (N, 8, 16))
    l = rng.integers(0, W, (N, 8, K)); share = np.repeat(rng.choice(np.array([0.0, 0.3, 0.6, 0.9]), (N, 8, PG)), R, axis=2)
    s = np.where(rng.random((N, 8, K)) < share, l, rng.integers(0, W, (N, 8, K)))
    c = rng.random((N, 8, K)); p = np.where(c < 0.3, s, np.where(c < 0.4, l, rng.integers(0, W, (N, 8, K))))
    return x, e, w, h, p, s, l, rng.integers(0, W, (N, 8, K))
def pack(x, e, w, h, p, s, l, q):
    r = {"xt": x.reshape(N, 128, W).astype(np.float32).astype(BF), "ed": e.reshape(N, 128, PG).astype(np.float32).astype(BF),
         "wt": np.ascontiguousarray(w.reshape(N, 128, 1)).astype(np.int32), "th": np.ascontiguousarray(h.reshape(N, 128, 1)).astype(np.int32)}
    for k, z in (("pl", p), ("sl", s), ("ll", l), ("ql", q)): r[k] = np.stack([gtable(a) for a in z])
    return r
def setup_inputs(rng):
    return pack(*parts(rng))
def setup_inputs_spread(rng):
    x, e, w, h, p, s, l, q = parts(rng)
    x = np.minimum((np.exp2(8 * rng.random((N, 8, 1, W))) * rng.random((N, 8, 16, W))).astype(np.int64), 255)
    e = np.minimum((np.exp2(8 * rng.random((N, 8, 1, PG))) * rng.random((N, 8, 16, PG))).astype(np.int64), 255)
    w = (16 * rng.random((N, 8, 16)) ** 3).astype(np.int64); h = np.minimum(np.exp2(12 * rng.random((N, 8, 16))).astype(np.int64) - 1, 4080)
    p, s, l, q = [(W * rng.random((N, 8, K)) ** 3).astype(np.int64) for z in range(4)]
    s = np.where(rng.random((N, 8, K)) < np.repeat(rng.random((N, 8, PG)), R, axis=2), l, s)
    return pack(x, e, w, h, p, s, l, q)
def setup_inputs_ends(rng):
    x = 255 * rng.integers(0, 2, (N, 8, 16, W)); e = 255 * rng.integers(0, 2, (N, 8, 16, PG)); w = 15 * rng.integers(0, 2, (N, 8, 16)); h = 4080 * rng.integers(0, 2, (N, 8, 16))
    kind = rng.integers(0, 3, (N, 8, 1)); kind[:, 7] = 0; kind[0, 0] = 0; kind[1, 1] = 1
    x[..., 0] = np.where(kind == 0, 0, np.where(kind == 1, 255, x[..., 0])); x[..., W - 1] = np.where(kind == 0, 255, np.where(kind == 1, 0, x[..., W - 1]))
    w[:, :, 5] = 0; w[:, 7] = 15; w[:, :, 2] = 15; w[:, :, 13] = 15
    h[:, :, 0] = 0; h[:, :, 15] = 0; h[:, :, 1] = 4080; h[:, :, 14] = 4080
    p, s, l, q = [np.where(rng.random((N, 8, K)) < 0.75, (W - 1) * rng.integers(0, 2, (N, 8, K)), rng.integers(0, W, (N, 8, K))) for z in range(4)]
    pv, sv, lv = [z.reshape(N, 8, PG, R) for z in (p, s, l)]; k = np.arange(R)
    for i in (0, 1, 2, 3, PG - 4, PG - 3, PG - 2, PG - 1):
        pv[:, :, i] = 0; sv[:, :, i] = W - 1; lv[:, :, i] = W - 1
    lv[:, :, [0, PG - 1]] = np.where(k % 4 == 1, 0, W - 1)
    lv[:, :, [1, PG - 2]] = np.where((k % 4 == 1) | (k == 2), 0, W - 1)
    lv[:, :, [3, PG - 4]] = 0
    e[..., [0, PG - 1]] = 0; e[:, :, 2, [0, PG - 1]] = 255; e[:, :, 13, [0, PG - 1]] = 18
    e[..., [2, PG - 3]] = 0; e[..., [3, PG - 4]] = 255
    return pack(x, e, w, h, p, s, l, q)
def setup_inputs_corners(rng):
    x, e, w, h, p, s, l, q = parts(rng)
    cnt = np.roll(np.array([31, 32, 0, 8 * PG, 33, 1, 8 * PG - 1, 64])[:N], int(rng.integers(0, N))); fl = np.zeros((N, 8 * PG), bool)
    for r in range(N): fl[r, rng.permutation(8 * PG)[:int(cnt[r])]] = True
    fr = np.repeat(fl.reshape(N, 8, PG), R, axis=2)
    lv = l.reshape(N, 8, PG, R); lv[:, :, [0, PG - 1]] = (W - 1) * rng.integers(0, 2, (N, 8, 2, R))
    far = (l + rng.integers(1, W, l.shape)) % W; half = np.repeat(rng.random((N, 8, PG)) < 0.5, R, axis=2)
    s = np.where(fr, far, l); p = np.where(fr | half, l, rng.integers(0, W, l.shape))
    for g in range(8):
        if g % 4 < 3: q[:, g] = (l, s, p)[g % 4][:, g]
    w[:, 0] = 0; w[:, 7] = 15; w[:, 4] = 15; w[:, 3] = 0; w[:, 3, 15] = 15; w[:, 5] = 0; w[:, 5, 0] = 1
    h = np.where(rng.random(h.shape) < 0.5, rng.choice(np.array([0, 1, 4079, 4080]), h.shape), h)
    e[..., [0, PG - 1]] = 0; e[:, :, 2, [0, PG - 1]] = 255; e[:, :, 13, [0, PG - 1]] = 18
    e[..., 1] = 255; e[..., PG - 2] = 0
    return pack(x, e, w, h, p, s, l, q)
def setup_inputs_alike(rng):
    x, e, w, h, p, s, l, q = parts(rng)
    step = rng.choice(np.array([1, 4, 8, 32]), (N, 8, 1, 1)); lane = rng.integers(0, 8, (N, 8, 16, 1))
    x = step * (rng.integers(0, 8, (N, 8, 1, W)) ^ lane); e = step * (rng.integers(0, 8, (N, 8, 1, PG)) ^ lane)
    h = step[..., 0] * rng.integers(20, 81, (N, 8, 16))
    return pack(x, e, w, h, p, s, l, q)
def setup_inputs_near(rng):
    x, e, w, h, p, s, l, q = parts(rng); n = np.arange(N); f = rng.integers(0, 16, N); k = np.arange(R)
    s[:, 0] = l[:, 0]; h[:, 0] = 0
    h[:, 7] = 4080; x[:, 7, :, :2] = 0; x[:, 7, :, W - 2:] = 255; x[n, 7, f, 1] = 1; x[n, 7, f, W - 2] = 254
    pv, sv, lv, qv = [z.reshape(N, 8, PG, R)[:, 7] for z in (p, s, l, q)]
    for z in (pv, sv, lv): z[:, PG - 1] = W - 1; z[:, PG - 3] = W - 1
    pv[:, PG - 1, R - 4:] = 0; sv[:, PG - 1, R - 4:] = 0; qv[:, PG - 1, R - 4:] = W - 2
    pv[:, PG - 2] = 0; sv[:, PG - 2] = W - 1; sv[:, PG - 2, 0] = W - 2; lv[:, PG - 2] = np.where(k % 4 == 1, 0, W - 1)
    e[:, 7, :, PG - 3] = 0; e[n, 7, f, PG - 3] = 1
    pv[:, PG - 4] = 1; sv[:, PG - 4] = 0; lv[:, PG - 4] = W - 1
    return pack(x, e, w, h, p, s, l, q)
def check_inputs(d):
    bad = []
    for k, hi in (("xt", 255), ("ed", 255), ("wt", 15), ("th", 4080), ("pl", W - 1), ("sl", W - 1), ("ll", W - 1), ("ql", W - 1)):
        v = np.asarray(d[k]).astype(np.float64)
        if not (np.min(v) >= 0 and np.max(v) <= hi): bad.append("range of " + k)
        elif np.any(v != np.floor(v)): bad.append("whole numbers of " + k)
    return bad
def dist(y, z):
    return np.add.reduce(np.abs(y - z), axis=1, dtype=np.int32)
def reference(xt, ed, wt, th, pl, sl, ll, ql):
    x = xt.astype(np.float32).astype(np.int16).reshape(N, 8, 16, W); e = ed.astype(np.float32).astype(np.int16).reshape(N, 8, 16, PG)
    w = wt.astype(np.int32).reshape(N, 8, 16, 1); h = th.astype(np.int32).reshape(N, 8, 16)[:, :, np.arange(K) % 16]
    p, s, l, q = [np.stack([gentries(a) for a in z]).astype(np.int64) for z in (pl, sl, ll, ql)]
    more = 37 * (np.arange(K) % R); A = np.zeros(N, np.int64)
    for t in range(V):
        new = np.zeros_like(l); failed = np.zeros((N, 8, PG), bool); m = np.zeros((N, 8, 16, PG), np.int16)
        for r in range(N):
            vp, vs, vl, vq = [np.take_along_axis(x[r], z[r][:, None, :], 2) for z in (p, s, l, q)]
            a = dist(vp, vs); b = dist(vs, vl); c = dist(vp, vl); d = dist(vq, vs); o = dist(vl, np.repeat(e[r], R, axis=2))
            failed[r] = 2 * np.sum((c - b).reshape(8, PG, R), axis=2) < np.sum(a.reshape(8, PG, R), axis=2)
            u = np.repeat(np.sum(w[r] * e[r], axis=1) & (W - 1), R, axis=1).astype(np.int64)
            change = ((l[r] * u >> 5) + l[r] + more + A[r]) & (W - 1)
            new[r] = np.where(np.repeat(failed[r], R, axis=1) & (c < b), p[r], np.where(d < b, q[r], np.where(o >= h[r], change, l[r])))
            m[r] = np.max(vl.reshape(8, 16, PG, R), axis=3)
        got = np.roll(m, N // 2, axis=0)
        e = np.where(failed[:, :, None, :], np.abs(e - got), (e + got) >> 1)
        A = np.sum(failed, axis=(1, 2)).astype(np.int64) & 31
        q = np.where(new != l, l, q); p, s, l = s, l, new
        if t < V - 1: p, s, l, q = [np.roll(z, H, axis=0) for z in (p, s, l, q)]
    out = [np.stack([gtable(a) for a in z]).astype(np.float32) for z in (p, s, l, q)]
    return {"yp": out[0], "ys": out[1], "yl": out[2], "yq": out[3], "ye": e.reshape(N, 128, PG).astype(np.float32).astype(BF)}

from concourse.mybir import AluOpType, AxisListType, ActivationFunctionType

W, PG, V, H, N = 4096, 192, 5, 5, 8
HP = 96
HC = HP * 16
NCH = 3
CH = HC // NCH
CO = CH // 16
TASKS = [(t, h) for t in range(V) for h in range(2)]

SCRATCH = {
    "X": ("sbuf", [128, W], "bfloat16"),
    "raw": ("sbuf", [128, 4 * PG], "int32"),
    "edit0": ("sbuf", [128, PG], "bfloat16"),
    "edit1": ("sbuf", [128, PG], "bfloat16"),
    "wraw": ("sbuf", [128, 1], "int32"),
    "traw": ("sbuf", [128, 1], "int32"),
    "wcol": ("sbuf", [128, 1], "float32"),
    "thi": ("sbuf", [128, 1], "int32"),
    "tlo": ("sbuf", [128, 1], "int32"),
    "thf": ("sbuf", [128, 1], "float32"),
    "tlf": ("sbuf", [128, 1], "float32"),
    "pidx": ("sbuf", [128, 1], "int32"),
    "kidx": ("sbuf", [128, 1], "int32"),
    "kcol": ("sbuf", [128, 1], "float32"),
    "acol": ("sbuf", [128, 1], "float32"),
    "aint": ("sbuf", [128, 1], "int32"),
    "amod": ("sbuf", [128, 1], "int32"),
    "one": ("sbuf", [128, 128], "bfloat16"),
    "ident": ("sbuf", [128, 128], "bfloat16"),
    "negid": ("sbuf", [128, 128], "bfloat16"),
    "half": ("sbuf", [128, 128], "bfloat16"),
    "blk": ("sbuf", [128, 128], "bfloat16"),
    "rep": ("sbuf", [128, 128], "bfloat16"),
    "wblk": ("sbuf", [128, 128], "bfloat16"),
    "sixt": ("sbuf", [128, 128], "float32"),
    "thr": ("sbuf", [128, 512], "bfloat16"),
    "thl": ("sbuf", [128, 128], "bfloat16"),
    "sel": ("sbuf", [128, 80], "bfloat16"),
    "mask": ("sbuf", [128, HC], "bfloat16"),
    "bk0": ("psum", [128, 512], "float32"),
    "bk1": ("psum", [128, 512], "float32"),
    "bk2": ("psum", [128, 512], "float32"),
    "bk3": ("psum", [128, 512], "float32"),
    "XS": ("psum", [128, 512], "float32"),
    "TR": ("psum", [128, 1024], "bfloat16"),
    "M6": ("psum", [128, 512], "float32"),
    "VB": ("psum", [128, 512], "float32"),
    "sgn": ("sbuf", [128, 384], "bfloat16"),
    "xs": ("sbuf", [128, 128], "float32"),
    "xf": ("sbuf", [128, 128], "bfloat16"),
    "xft": ("sbuf", [128, HP], "bfloat16"),
    "PQ": ("sbuf", [128, 2 * HP], "float32"),
    "Qf": ("sbuf", [128, HP], "float32"),
    "GK": ("sbuf", [128, HP], "float32"),
    "KK": ("sbuf", [128, 2 * HP], "float32"),
    "m1": ("sbuf", [128, HP], "float32"),
    "m2": ("sbuf", [128, HP], "float32"),
    "mi": ("sbuf", [128, HP], "int32"),
    "ti": ("sbuf", [128, HP], "int32"),
    "fi": ("sbuf", [128, HP], "int32"),
    "NQ": ("sbuf", [128, 2 * HP], "int32"),
    "ne": ("sbuf", [128, HP], "float32"),
    "ad": ("sbuf", [128, HP], "float32"),
    "av": ("sbuf", [128, HP], "int32"),
    "df": ("sbuf", [128, HP], "float32"),
    "ui": ("sbuf", [128, HP], "int32"),
    "ub": ("sbuf", [128, PG], "int32"),
    "cnt": ("sbuf", [128, 2], "float32"),
    "of0": ("sbuf", [128, 4 * HP], "float32"),
    "of1": ("sbuf", [128, 4 * HP], "float32"),
}
for _h in range(2):
    for _n in ("s", "l", "lp", "d1", "dq", "ga", "gb", "gc", "gd", "go", "run"):
        SCRATCH["%s_%d" % (_n, _h)] = ("sbuf", [128, HC], "bfloat16")
for _t in range(V):
    SCRATCH["ml%d" % _t] = ("sbuf", [128, PG], "bfloat16")
    for _h in range(2):
        SCRATCH["land%d%d" % (_t, _h)] = ("sbuf", [128, 4 * HP], "uint16")
        SCRATCH["ms%d%d" % (_t, _h)] = ("sbuf", [128, HP], "bfloat16")
        if _t < V - 1:
            SCRATCH["nq%d%d" % (_t, _h)] = ("sbuf", [128, 2 * HP], "uint16")

ORDER = """l0 p0 sg p1 p2 B0 l1 em a1 tr b0 pt tf ea cf a0 B1 early l2 sf B2 a2 C0 ca cb cc b1 max O0 C1 thr c0 me b2 en C2 q0 s0 q1 s1
O1 O2 um am o1 uv o0 c1 o2 q2 av Sa c2 O3 d0 o3 d1 d2 Sb Sc s2 So pa pb Sd""".split()

L_ON_SCALAR = [(0, 0), (1, 0), (1, 1)]

LOADS = ["lx0", "lx1", "lp", "ls", "ll", "lq", "le", "lw", "lt"]
SEMAPHORES = ["qv", "qs", "qt", "qg", "sent", "oy", "os"] + LOADS
for _t in range(V):
    for _h in range(2):
        SEMAPHORES.append("am%d%d" % (_t, _h))
        if _t:
            SEMAPHORES += ["ae%d%d" % (_t, _h), "an%d%d" % (_t, _h)]


def rank_program(g, core, T, topo):
    rank = T.rank_of(core)
    if rank is None:
        return
    Op, Act = AluOpType, ActivationFunctionType
    queue = {"v": g.vector, "s": g.scalar, "t": g.tensor, "g": g, "y": g.sync}
    count = {e: 0 for e in queue}
    known = {e: {} for e in queue}
    last, seen, bank = {}, {}, {}
    seq = [0]
    total = {}

    def add(sem, n):
        total[sem] = total.get(sem, 0) + n
        return total[sem]

    def wait_for(e, deps):
        for d in sorted(deps, key=lambda d: -d[0]):
            if known[e].get(d[1], 0) < d[2]:
                queue[e].wait_ge(T.sem[d[1]], d[2])
                for s, v in list(d[3].items()) + [(d[1], d[2])]:
                    if known[e].get(s, 0) < v:
                        known[e][s] = v

    def gather_deps(e, rd, wr, bk):
        deps = []
        for k in rd:
            deps += last[k]
        for k in wr:
            deps += last.get(k, []) + list(seen.get(k, {}).values())
        for b in bk:
            deps += [x for f, x in bank.get(b, {}).items() if f != e]
        return deps

    def note(e, rd, wr, bk, tok):
        for k in rd:
            seen.setdefault(k, {})[e] = tok
        for k in wr:
            last[k] = [tok]
            seen[k] = {}
        for b in bk:
            bank.setdefault(b, {})[e] = tok

    def token(e, sem, val):
        seq[0] += 1
        clock = dict(known[e])
        clock[sem] = val
        return (seq[0], sem, val, clock)

    def op(e, rd, wr, bk, ins):
        wait_for(e, gather_deps(e, rd, wr, bk))
        sem = "q" + e
        ins(queue[e]).then_inc(T.sem[sem], 1)
        note(e, rd, wr, bk, token(e, sem, add(sem, 1)))

    def dma(e, rd, wr, sem, out, in_):
        wait_for(e, gather_deps(e, rd, wr, ()))
        queue[e].dma_start(out, in_).then_inc(T.sem[sem], 16)
        note(e, rd, wr, (), token(e, sem, add(sem, 16)))

    def send(rd, dst, out, in_, sem):
        wait_for("g", gather_deps("g", rd, (), ()))
        rid, pid = topo.addr(dst, core)
        g.remote_dma(out, in_, T.sem[sem], T.sem.sent, pid, rid, topo.mask(core, dst))
        add("sent", len(topo.engines(core, dst)))
        note("g", rd, (), (), token("g", "sent", total["sent"]))

    def lands(key, sem, src):
        n = len(topo.engines(src, core))
        add(sem, n)
        last[key] = [(0, sem, n, {})]

    nxt, prv = T.cores[(rank + H) % N], T.cores[(rank - H) % N]
    opp = T.cores[(rank + N // 2) % N]
    for t, h in TASKS:
        lands(("ml", t, h), "am%d%d" % (t, h), opp)
        if t:
            lands(("early", t, h), "ae%d%d" % (t, h), prv)
            lands(("late", t, h), "an%d%d" % (t, h), prv)

    R = T.raw
    dma("y", [], ["raw1"], "ls", R[:, PG:2 * PG], T.sl[:])
    dma("s", [], ["raw0"], "lp", R[:, 0:PG], T.pl[:])
    dma("y", [], ["X0"], "lx0", T.X[:, 0:W // 2], T.xt[:, 0:W // 2])
    dma("s", [], ["X1"], "lx1", T.X[:, W // 2:W], T.xt[:, W // 2:W])
    dma("y", [], ["raw2"], "ll", R[:, 2 * PG:3 * PG], T.ll[:])
    dma("s", [], ["raw3"], "lq", R[:, 3 * PG:4 * PG], T.ql[:])
    dma("y", [], [("E", 0, 0), ("E", 0, 1)], "le", T.edit0[:], T.ed[:])
    dma("y", [], ["wraw"], "lw", T.wraw[:], T.wt[:])
    dma("s", [], ["traw"], "lt", T.traw[:], T.th[:])

    op("v", [], ["one"], (), lambda q: q.memset(T.one[:], 1.0))
    grid = [[-16, 8], [0, 16]]
    op("g", ["one"], ["ident"], (), lambda q: q.affine_select(T.ident[:], T.one[:], [[-1, 128]], Op.is_equal, 0.0, 0, 1))
    op("g", ["one"], ["half"], (), lambda q: q.affine_select(T.half[:], T.one[:], grid, Op.is_ge, 0.0, 0, 1))
    op("g", ["half"], ["blk"], (), lambda q: q.affine_select(T.blk[:], T.half[:], [[16, 8], [0, 16]], Op.is_ge, 0.0, 15, -1))
    op("g", ["one"], ["rep"], (), lambda q: q.affine_select(T.rep[:], T.one[:], grid, Op.is_equal, 0.0, -15, 1))
    op("g", [], ["pidx"], (), lambda q: q.iota(T.pidx[:], [[0, 1]], 0, 1))
    op("v", [], ["sel"], (), lambda q: q.memset(T.sel[:], 0.0))
    op("v", [], ["thr"], (), lambda q: q.memset(T.thr[:], 0.0))
    op("v", [], ["sixt"], (), lambda q: q.memset(T.sixt[:], 0.0625))
    op("v", [], ["acol"], (), lambda q: q.memset(T.acol[:], 0.0))
    op("v", [], ["mask"], (), lambda q: q.memset(T.mask[:], 1.0))
    op("v", [], ["mask"], (), lambda q: q.memset(T.mask[:, 0::16], 0.0))

    def land(t, h):
        return T["land%d%d" % (t, h)]

    def convert(h):
        L = land(0, h)
        for z in (1, 2, 0, 3):
            op("v", ["raw%d" % z], [("land", z, h)], (), lambda q: q.tensor_copy(
                L[:, z * HP:(z + 1) * HP], R[:, z * PG + h * HP:z * PG + (h + 1) * HP]))

    def lk(t, h, z):
        return ("land", z, h) if t == 0 else (("early" if z < 2 else "late"), t, h)

    def off(t, h, z, c):
        return land(t, h)[:, z * HP + c * CO:z * HP + (c + 1) * CO]

    def sl_(c):
        return slice(c * CH, (c + 1) * CH)

    def s_gather(t, h, c):
        op("s", ["X0", "X1", lk(t, h, 1)], [("s", h, c)], (), lambda q: q.activation(
            T["s_%d" % h][:, sl_(c)], T.X[:, 0:W].indirect(off(t, h, 1, c)), Act.Copy))

    def l_gather(t, h, c):
        out, in_ = T["l_%d" % h][:, sl_(c)], T.X[:, 0:W].indirect(off(t, h, 2, c))
        if (h, c) in L_ON_SCALAR:
            op("s", ["X0", "X1", lk(t, h, 2)], [("l", h, c)], (), lambda q: q.activation(out, in_, Act.Copy))
        else:
            op("v", ["X0", "X1", lk(t, h, 2)], [("l", h, c)], (), lambda q: q.tensor_copy(out, in_))

    def d_gather(t, h, c, z, name):
        op("v", ["X0", "X1", lk(t, h, z), ("s", h, c)], [(name, h, c)], (), lambda q: q.tensor_tensor(
            T["%s_%d" % (name, h)][:, sl_(c)], T.X[:, 0:W].indirect(off(t, h, z, c)), T["s_%d" % h][:, sl_(c)], Op.subtract))

    def abs_sb(h, c, src, dst):
        op("s", [(src, h, c)], [(dst, h, c)], (), lambda q: q.activation(
            T["%s_%d" % (dst, h)][:, sl_(c)], T["%s_%d" % (src, h)][:, sl_(c)], Act.Abs))

    def abs_ps(h, c, dst):
        op("s", [], [(dst, h, c)], ["bk%d" % c], lambda q: q.activation(
            T["%s_%d" % (dst, h)][:, sl_(c)], T["bk%d" % c][:], Act.Abs))

    def mm(bk, out, lhsT, rhs, start, stop, rd):
        op("t", rd, [], [bk], lambda q: q.matmul(out, lhsT, rhs, start, stop))

    def diff_ls(h, c):
        b = "bk%d" % c
        mm(b, T[b][:], T.ident[:], T["l_%d" % h][:, sl_(c)], True, False, ["ident", ("l", h, c)])
        mm(b, T[b][:], T.negid[:], T["s_%d" % h][:, sl_(c)], False, True, ["negid", ("s", h, c)])

    def diff_lp(h, c):
        b = "bk%d" % c
        op("v", [("d1", h, c)], [("lp", h, c)], [b], lambda q: q.tensor_tensor(
            T["lp_%d" % h][:, sl_(c)], T[b][:], T["d1_%d" % h][:, sl_(c)], Op.subtract))

    def diff_le(t, h, i):
        b = "bk%d" % ((i + 3) % 4)
        lall = [("l", h, c) for c in range(NCH)]
        for j in range(4):
            out = T[b][:, j * HP:(j + 1) * HP]
            mm(b, out, T.ident[:], T["l_%d" % h][:, 4 * i + j::16], True, False, ["ident"] + lall)
            mm(b, out, T.negid[:], T["edit%d" % (t % 2)][:, h * HP:(h + 1) * HP], False, True, ["negid", ("E", t % 2, h)])

    def abs_le(h, i):
        b = "bk%d" % ((i + 3) % 4)
        op("s", [], [("go", h, i)], [b], lambda q: q.activation(
            T["go_%d" % h][:, i * 4 * HP:(i + 1) * 4 * HP], T[b][:, 0:4 * HP], Act.Abs))

    def sum_start(h):
        mm("XS", T.XS[0:HP, :], T.one[:, 0:HP], T.thr[:], True, False, ["one", "thr"])
        mm("XS", T.XS[0:HP, 256:384], T.one[:, 0:HP], T.thl[:], False, False, ["thl"])

    def sums(h, kind, end=False):
        D = T["g%s_%d" % (kind, h)]
        rd = ["sel"] + [("g" + kind, h, c) for c in range(4 if kind == "o" else NCH)]
        for k in range(16):
            left = D[:, k * HP:(k + 1) * HP] if kind == "o" else D[:, k::16]
            if kind == "b":
                out, right = T.XS[0:HP, k::16], T.sel[:, 0:32]
            elif kind == "c":
                out, right = T.XS[0:HP, k::16], T.sel[:, 32:64]
            else:
                y = {"d": 1, "o": 2, "a": 3}[kind]
                out = T.XS[0:HP, y * 128 + k:(y + 1) * 128:16]
                right = T.sel[:, 72:80] if kind == "d" else T.sel[:, 64:72]
            mm("XS", out, left, right, False, bool(end and k == 15), rd)

    def run_max(t, h):
        op("v", ["mask"] + [("l", h, c) for c in range(NCH)], [("run", h)], (), lambda q: q.tensor_tensor_scan(
            T["run_%d" % h][:], T.mask[:], T["l_%d" % h][:], 0.0, Op.mult, Op.max))
        ms = T["ms%d%d" % (t, h)]
        op("v", [("run", h)], [("ms", t, h)], (), lambda q: q.tensor_copy(ms[:], T["run_%d" % h][:, 15::16]))
        send([("ms", t, h)], opp, T["ml%d" % t][:, h * HP:(h + 1) * HP], ms[:], "am%d%d" % (t, h))

    def tt(rd, wr, bk, out, a, b, o):
        op("v", rd, wr, bk, lambda q: q.tensor_tensor(out, a, b, o))

    VB, M6, TR = T.VB, T.M6, T.TR
    vLf, vLQ, vK3, vK1, vLK = [VB[:, i * HP:(i + 1) * HP] for i in range(5)]

    def pre_a(t, h):
        L = land(t, h)
        op("v", [lk(t, h, 2)], ["vLf"], ["VB"], lambda q: q.tensor_copy(vLf, L[:, 2 * HP:3 * HP]))
        op("v", [lk(t, h, 3)], ["Qf"], (), lambda q: q.tensor_copy(T.Qf[:], L[:, 3 * HP:4 * HP]))
        op("s", ["Qf"], ["Q2"], (), lambda q: q.activation(T.PQ[:, HP:2 * HP], T.Qf[:], Act.Copy, bias=float(2 ** 20)))
        tt(["ub%d" % h, "vLf"], ["ti"], ["VB"], T.ti[:], T.ub[:, h * HP:(h + 1) * HP], vLf, Op.mult)
        op("v", [lk(t, h, 0)], ["P2"], (), lambda q: q.tensor_scalar(
            T.PQ[:, 0:HP], L[:, 0:HP], float(2 ** 21), None, Op.add))

    def pre_b(t, h):
        L = land(t, h)
        op("v", ["ti"], ["fi"], (), lambda q: q.tensor_scalar(T.fi[:], T.ti[:], 5, None, Op.arith_shift_right))
        op("v", [lk(t, h, 2), "kcol", "acol"], ["vLK"], ["VB"], lambda q: q.tensor_scalar(
            vLK, L[:, 2 * HP:3 * HP], T.kcol[:], T.acol[:], Op.add, Op.add))
        tt(["vLf", "Qf"], ["vLQ"], ["VB"], vLQ, vLf, T.Qf[:], Op.subtract)
        tt(["fi", "vLK"], ["GK"], ["VB"], T.GK[:], T.fi[:], vLK, Op.add)

    def sign(h):
        op("s", [], ["sgn"], ["XS"], lambda q: q.activation(T.sgn[0:HP, :], T.XS[0:HP, 0:384], Act.Sign))

    def page_test(h):
        op("v", ["mask"], ["xs"], ["XS"], lambda q: q.tensor_tensor_scan(
            T.xs[0:HP, :], T.mask[0:HP, 0:128], T.XS[0:HP, 384:512], 0.0, Op.mult, Op.add))
        op("v", ["xs"], ["xf"], (), lambda q: q.tensor_scalar(T.xf[0:HP, :], T.xs[0:HP, :], 0.0, None, Op.is_gt))

    def turn(h):
        for y in range(3):
            op("t", ["sgn", "ident"], [], ["TR"], lambda q: q.transpose(
                TR[:, y * HP:(y + 1) * HP], T.sgn[0:HP, y * 128:(y + 1) * 128], T.ident[0:HP, 0:HP]))

    def turn_fail(h):
        op("t", ["xf", "ident"], [], ["TR"], lambda q: q.transpose(TR[:, 384:384 + HP], T.xf[0:HP, :], T.ident[0:HP, 0:HP]))

    def copy_fail(h):
        op("s", [], ["xft"], ["TR"], lambda q: q.activation(T.xft[:], TR[:, 384:384 + HP], Act.Copy))

    def spread_fail(h):
        mm("M6", M6[:, 0:HP], T.rep[:], T.xft[:], True, True, ["rep", "xft"])

    def choose_a(t, h):
        tt(["P2", "Q2"], ["KK"], ["TR"], T.KK[:], TR[:, 0:2 * HP], T.PQ[:], Op.mult)
        tt(["GK"], ["vK3"], ["TR", "VB"], vK3, TR[:, 2 * HP:3 * HP], T.GK[:], Op.mult)
        tt(["KK", "vK3"], ["m1"], ["VB"], T.m1[:], T.KK[:, HP:2 * HP], vK3, Op.max)

    def choose_b(t, h):
        tt(["KK"], ["vK1"], ["M6", "VB"], vK1, T.KK[:, 0:HP], M6[:, 0:HP], Op.mult)
        tt(["m1", "vLf"], ["m2"], ["VB"], T.m2[:], T.m1[:], vLf, Op.max)
        tt(["m2", "vK1"], ["mi"], ["VB"], T.mi[:], T.m2[:], vK1, Op.max)
        op("v", ["mi"], ["NQ0"], (), lambda q: q.tensor_scalar(T.NQ[:, 0:HP], T.mi[:], 4095, None, Op.bitwise_and))
        tt(["NQ0", "vLf"], ["ne"], ["VB"], T.ne[:], T.NQ[:, 0:HP], vLf, Op.not_equal)

    def choose_c(t, h):
        tt(["ne", "vLQ"], ["vK1"], ["VB"], vK1, T.ne[:], vLQ, Op.mult)
        tt(["Qf", "vK1"], ["NQ1"], ["VB"], T.NQ[:, HP:2 * HP], T.Qf[:], vK1, Op.add)
        if t < V - 1:
            n = T["nq%d%d" % (t, h)]
            op("v", ["NQ0", "NQ1"], [("nq", t, h)], (), lambda q: q.tensor_copy(n[:], T.NQ[:]))
            send([("nq", t, h)], nxt, land(t + 1, h)[:, 2 * HP:4 * HP], n[:], "an%d%d" % (t + 1, h))
        else:
            o = T["of%d" % h]
            op("v", ["NQ0", "NQ1"], [("of", h, 1)], (), lambda q: q.tensor_copy(o[:, 2 * HP:4 * HP], T.NQ[:]))
            c = slice(h * HP, (h + 1) * HP)
            dma("y", [("of", h, 1)], [], "oy", T.yl[:, c], o[:, 2 * HP:3 * HP])
            dma("y", [("of", h, 1)], [], "oy", T.yq[:, c], o[:, 3 * HP:4 * HP])

    def early(t, h):
        L = land(t, h)
        if t < V - 1:
            send([lk(t, h, 1), lk(t, h, 2)], nxt, land(t + 1, h)[:, 0:2 * HP], L[:, HP:3 * HP], "ae%d%d" % (t + 1, h))
        else:
            o = T["of%d" % h]
            op("v", [lk(t, h, 1), lk(t, h, 2)], [("of", h, 0)], (), lambda q: q.tensor_copy(o[:, 0:2 * HP], L[:, HP:3 * HP]))
            c = slice(h * HP, (h + 1) * HP)
            dma("y", [("of", h, 0)], [], "oy", T.yp[:, c], o[:, 0:HP])
            dma("y", [("of", h, 0)], [], "oy", T.ys[:, c], o[:, HP:2 * HP])

    def edit_mm(t, h):
        E, m = T["edit%d" % (t % 2)][:, h * HP:(h + 1) * HP], T["ml%d" % t][:, h * HP:(h + 1) * HP]
        mm("M6", M6[:, HP:2 * HP], T.ident[:], E, True, False, ["ident", ("E", t % 2, h)])
        mm("M6", M6[:, HP:2 * HP], T.negid[:], m, False, True, ["negid", ("ml", t, h)])
        mm("M6", M6[:, 2 * HP:3 * HP], T.ident[:], E, True, False, [])
        mm("M6", M6[:, 2 * HP:3 * HP], T.ident[:], m, False, True, [])

    def edit_abs(h):
        op("s", [], ["ad"], ["M6"], lambda q: q.activation(T.ad[:], M6[:, HP:2 * HP], Act.Abs))

    def edit_mean(h):
        op("v", [], ["av"], ["M6"], lambda q: q.tensor_scalar(T.av[:], M6[:, 2 * HP:3 * HP], 0.5, -0.25, Op.mult, Op.add))
        tt(["ad", "av"], ["df"], (), T.df[:], T.ad[:], T.av[:], Op.subtract)

    def edit_new(t, h):
        tt(["df"], ["vK1"], ["M6", "VB"], vK1, T.df[:], M6[:, 0:HP], Op.mult)
        E = T["edit%d" % ((t + 1) % 2)]
        tt(["av", "vK1"], [("E", (t + 1) % 2, h)], ["VB"], E[:, h * HP:(h + 1) * HP], T.av[:], vK1, Op.add)
        if t < V - 1:
            op("v", [], ["cnt%d" % h], ["M6"], lambda q: q.tensor_reduce(T.cnt[:, h:h + 1], M6[:, 0:HP], AxisListType.X, Op.add))
        else:
            dma("y", [("E", (t + 1) % 2, h)], [], "oy", T.ye[:, h * HP:(h + 1) * HP], E[:, h * HP:(h + 1) * HP])

    def u_mm(t, h):
        mm("M6", M6[:, 3 * HP:4 * HP], T.wblk[:], T["edit%d" % (t % 2)][:, h * HP:(h + 1) * HP], True, True, ["wblk", ("E", t % 2, h)])

    def u_mod(h):
        op("v", [], ["ui"], ["M6"], lambda q: q.tensor_copy(T.ui[:], M6[:, 3 * HP:4 * HP]))
        op("v", ["ui"], ["ub%d" % h], (), lambda q: q.tensor_scalar(
            T.ub[:, h * HP:(h + 1) * HP], T.ui[:], 4095, None, Op.bitwise_and))

    def a_mm():
        mm("M6", M6[:, 384:385], T.sixt[:], T.cnt[:, 0:1], True, False, ["sixt", "cnt0"])
        mm("M6", M6[:, 384:385], T.sixt[:], T.cnt[:, 1:2], False, True, ["cnt1"])

    def a_mod():
        op("v", [], ["aint"], ["M6"], lambda q: q.tensor_copy(T.aint[:], M6[:, 384:385]))
        op("v", ["aint"], ["amod"], (), lambda q: q.tensor_scalar(T.amod[:], T.aint[:], 31, None, Op.bitwise_and))
        op("v", ["amod"], ["acol"], (), lambda q: q.tensor_copy(T.acol[:], T.amod[:]))

    convert(0)
    convert(1)
    for h in range(2):
        early(0, h)
    for c in range(NCH):
        s_gather(0, 0, c)
    op("v", ["ident"], ["negid"], (), lambda q: q.tensor_scalar(T.negid[:], T.ident[:], -1.0, None, Op.mult))
    for c0, f in ((0, 1.0), (8, 1.0), (24, 2.0), (32, -1.0), (56, -2.0), (64, 1.0), (72, -1.0)):
        op("v", ["blk"], ["sel"], (), lambda q: q.tensor_scalar(T.sel[:, c0:c0 + 8], T.blk[:, 0::16], f, None, Op.mult))
    op("v", ["wraw"], ["wcol"], (), lambda q: q.tensor_copy(T.wcol[:], T.wraw[:]))
    op("v", ["traw"], ["thi"], (), lambda q: q.tensor_scalar(T.thi[:], T.traw[:], 4, None, Op.arith_shift_right))
    op("v", ["traw"], ["tlo"], (), lambda q: q.tensor_scalar(T.tlo[:], T.traw[:], 15, None, Op.bitwise_and))
    op("v", ["pidx"], ["kidx"], (), lambda q: q.tensor_scalar(T.kidx[:], T.pidx[:], 15, None, Op.bitwise_and))
    op("v", ["blk", "wcol"], ["wblk"], (), lambda q: q.tensor_scalar(T.wblk[:], T.blk[:], T.wcol[:], None, Op.mult))
    op("v", ["thi"], ["thf"], (), lambda q: q.tensor_scalar(T.thf[:], T.thi[:], -16.0, None, Op.mult))
    op("v", ["tlo"], ["tlf"], (), lambda q: q.tensor_scalar(T.tlf[:], T.tlo[:], -1.0, 0.5, Op.mult, Op.add))
    op("v", ["kidx"], ["kcol"], (), lambda q: q.tensor_scalar(T.kcol[:], T.kidx[:], 37.0, 4096.0, Op.mult, Op.add))
    op("v", ["ident", "thf"], ["thr"], (), lambda q: q.tensor_scalar(T.thr[:, 256:384], T.ident[:], T.thf[:], None, Op.mult))
    op("v", ["ident", "tlf"], ["thl"], (), lambda q: q.tensor_scalar(T.thl[:], T.ident[:], T.tlf[:], None, Op.mult))
    for h in range(2):
        u_mm(0, h)
        u_mod(h)

    def goes_on(t):
        return t < V - 1

    here = {
        "early": lambda t, h: early(t, h) if t else None,
        "thr": lambda t, h: sum_start(h),
        "max": lambda t, h: run_max(t, h),
        "pa": lambda t, h: pre_a(t, h),
        "pb": lambda t, h: pre_b(t, h),
        "Sa": lambda t, h: sums(h, "a"),
        "Sb": lambda t, h: sums(h, "b"),
        "Sc": lambda t, h: sums(h, "c"),
        "So": lambda t, h: sums(h, "o"),
        "Sd": lambda t, h: sums(h, "d", True),
    }
    for c in range(NCH):
        here["p%d" % c] = lambda t, h, c=c: d_gather(t, h, c, 0, "d1")
        here["q%d" % c] = lambda t, h, c=c: d_gather(t, h, c, 3, "dq")
        here["l%d" % c] = lambda t, h, c=c: l_gather(t, h, c)
        here["a%d" % c] = lambda t, h, c=c: abs_sb(h, c, "d1", "ga")
        here["d%d" % c] = lambda t, h, c=c: abs_sb(h, c, "dq", "gd")
        here["b%d" % c] = lambda t, h, c=c: abs_ps(h, c, "gb")
        here["c%d" % c] = lambda t, h, c=c: abs_sb(h, c, "lp", "gc")
        here["B%d" % c] = lambda t, h, c=c: diff_ls(h, c)
        here["C%d" % c] = lambda t, h, c=c: diff_lp(h, c)
    for i in range(4):
        here["O%d" % i] = lambda t, h, i=i: diff_le(t, h, i)
        here["o%d" % i] = lambda t, h, i=i: abs_le(h, i)
    back = {
        "sg": lambda t, h: sign(h),
        "tr": lambda t, h: turn(h),
        "pt": lambda t, h: page_test(h),
        "tf": lambda t, h: turn_fail(h),
        "cf": lambda t, h: copy_fail(h),
        "em": lambda t, h: edit_mm(t, h),
        "ea": lambda t, h: edit_abs(h),
        "sf": lambda t, h: spread_fail(h),
        "ca": lambda t, h: choose_a(t, h),
        "cb": lambda t, h: choose_b(t, h),
        "cc": lambda t, h: choose_c(t, h),
        "me": lambda t, h: edit_mean(h),
        "en": lambda t, h: edit_new(t, h),
        "um": lambda t, h: u_mm(t + 1, h) if goes_on(t) else None,
        "uv": lambda t, h: u_mod(h) if goes_on(t) else None,
        "am": lambda t, h: a_mm() if goes_on(t) and h else None,
        "av": lambda t, h: a_mod() if goes_on(t) and h else None,
    }
    ahead = {"s%d" % c: (lambda t, h, c=c: s_gather(t, h, c)) for c in range(NCH)}
    for i in range(len(TASKS) + 1):
        for step in ORDER:
            for table, j in ((here, i), (back, i - 1), (ahead, i + 1)):
                if step in table and 0 <= j < len(TASKS):
                    table[step](*TASKS[j])
    for sem in sorted(total):
        if known["g"].get(sem, 0) < total[sem]:
            g.wait_ge(T.sem[sem], total[sem])
